import numpy as np
CORES = [24,48,72,152,176,200]
N = 6
TK = 128
D = 128 * N
EPS = 0.01
def setup_inputs(rng):
    return {"x": rng.standard_normal((N, 128, TK), dtype=np.float32) * (0.5 + np.abs(rng.standard_normal((1, 1, TK), dtype=np.float32))), "v": rng.standard_normal((N, 128, TK), dtype=np.float32) * (0.5 + np.abs(rng.standard_normal((1, 1, TK), dtype=np.float32)))}
def setup_inputs_big(rng):
    d = setup_inputs(rng)
    for k in ("x", "v"): d[k] = (d[k].astype(np.float32) * 1024.0).astype(d[k].dtype)
    return d
def setup_inputs_small(rng):
    d = setup_inputs(rng)
    for k in ("x",): d[k] = (d[k].astype(np.float32) * (1 / 1024.0)).astype(d[k].dtype)
    return d
def setup_inputs_apart(rng):
    d = setup_inputs(rng)
    f = (10.0 ** rng.permutation(np.linspace(-1.5, 1.5, N))).astype(np.float32).reshape(N, 1, 1)
    for k in ("x", "v"): d[k] = (d[k].astype(np.float32) * f).astype(d[k].dtype)
    return d
def setup_inputs_mixed(rng):
    d = setup_inputs(rng)
    for k in ("x", "v"):
        f = (10.0 ** rng.uniform(-3, 3, (1, 1, TK))).astype(np.float32); shape = rng.integers(3, size=(1, 1, TK))
        x = d[k].astype(np.float32)
        m = x.mean(axis=(0, 1), keepdims=True); level = m + np.sign(x - m) * np.abs(x - m).mean(axis=(0, 1), keepdims=True) * rng.uniform(0.9, 1.1, x.shape).astype(np.float32)
        other = x * np.where(rng.random(x.shape) < 0.5, 0.1, 1.0).astype(np.float32)
        d[k] = (np.where(shape == 1, level, np.where(shape == 2, other, x)) * f).astype(d[k].dtype)
    return d
def reference(x, v):
    X, V = x.astype(np.float64), v.astype(np.float64)
    n = X / np.sqrt((X ** 2).sum(axis=(0, 1)) / D + EPS)
    Z = n + V
    return {"y": (Z / np.sqrt((Z ** 2).sum(axis=(0, 1)) / D + EPS)).astype(np.float32)}

@@ -1,0 +1,209 @@
+from concourse.bass import DstId, RemoteDMATransfer
+from concourse.mybir import AluOpType, AxisListType, ActivationFunctionType
+
+N = 6
+D = 128 * N
+EPS = 0.01
+SIM_CORES = 256
+K_ENG = 8
+PER_HELPER = 2
+
+SCRATCH = {
+    "xs": ("sbuf", [128, 128], "float32"),
+    "vs": ("sbuf", [128, 128], "float32"),
+    "pr": ("sbuf", [128, 384], "float32"),
+    "wd": ("sbuf", [128, 2], "float32"),
+    "ones": ("sbuf", [128, 128], "float32"),
+    "ident": ("sbuf", [128, 128], "float32"),
+    "landA": ("sbuf", [128, 4 * N], "float32"),
+    "landB": ("sbuf", [128, 4 * N], "float32"),
+    "col": ("sbuf", [128, 32], "float32"),
+    "xr": ("sbuf", [128, 128], "float32"),
+    "zt": ("sbuf", [128, 128], "float32"),
+    "dg": ("sbuf", [128, 128], "float32"),
+    "ys": ("sbuf", [128, 128], "float32"),
+    "psa": ("psum", [128, 512], "float32"),
+    "psb": ("psum", [128, 512], "float32"),
+    "pxt": ("psum", [128, 512], "float32"),
+    "pvt": ("psum", [128, 512], "float32"),
+    "pya": ("psum", [128, 512], "float32"),
+    "pyb": ("psum", [128, 512], "float32"),
+}
+SEMAPHORES = ["ldx", "ldv", "cw", "cone", "cid", "pxx", "pxv", "pvv", "sta", "stb", "minea", "mineb", "tx", "tv",
+              "arra", "arrb", "sent", "m1", "a1", "q1", "qh1", "c2", "mv", "mve", "s1", "u1", "g1", "r1", "xrs", "tt", "a2",
+              "q2", "s2", "sh2", "u2", "w2", "zs", "dgs", "ya", "yb", "ca", "cb", "out"]
+
+
+def _low_bits(mask, k):
+    got, bit = 0, 1
+    while k > 0:
+        if mask & bit:
+            got |= bit
+            k -= 1
+        bit <<= 1
+    return got
+
+
+def _plan(rank_core, cores, topo):
+    others = [d for d in cores if d != rank_core]
+    direct = [d for d in others if topo.may_write(rank_core, d)]
+    cross = [d for d in others if not topo.may_write(rank_core, d)]
+    cand = [c for c in range(SIM_CORES)
+            if c not in cores and topo.host(c) == topo.host(rank_core) and topo.chip(c) == topo.chip(rank_core)
+            and all(topo.may_write(c, d) for d in cross)]
+    cand.sort(key=lambda c: (topo.die(c) != topo.die(rank_core), c))
+    groups = [cross[i:i + PER_HELPER] for i in range(0, len(cross), PER_HELPER)]
+    return direct, [(cand[i], grp) for i, grp in enumerate(groups)]
+
+
+def _send(g, T, topo, core, dests, ap, sem):
+    m = topo.mask(core, dests[0])
+    for d in dests:
+        m &= topo.mask(core, d)
+    m = _low_bits(m, K_ENG)
+    ids = []
+    for d in dests:
+        rid, pid = topo.addr(d, core)
+        ids.append(DstId(rid=rid, pnc=pid))
+    g.remote_dma_fused([RemoteDMATransfer(dst_ids=ids, dma_engine_mask=m, remote_sem=sem, srcs=[ap],
+                                          dsts=[ap for _ in dests], alu_op=0)], local_sem=T.sem.sent)
+    return K_ENG
+
+
+def rank_program(g, core, T, topo):
+    S = T.sem
+    cores = list(T.cores)
+    rank = T.rank_of(core)
+    if rank is None:
+        for r, rc in enumerate(cores):
+            for h, grp in _plan(rc, cores, topo)[1]:
+                if h == core:
+                    sent = 0
+                    g.wait_ge(S.arra, K_ENG)
+                    sent += _send(g, T, topo, core, grp, T.landA[:, 4 * r:4 * r + 1], S.arra)
+                    g.wait_ge(S.arrb, K_ENG)
+                    sent += _send(g, T, topo, core, grp, T.landB[:, 4 * r:4 * r + 2], S.arrb)
+                    g.wait_ge(S.sent, sent)
+        return
+
+    A, F, X = AluOpType, ActivationFunctionType, AxisListType.X
+    V, P, C, Y = g.vector, g.tensor, g.scalar, g.sync
+    direct, helpers = _plan(core, cores, topo)
+    names = ["m1", "a1", "q1", "qh1", "c2", "mv", "mve", "s1", "u1", "g1", "r1", "tt", "a2", "q2", "s2", "sh2", "u2", "w2"]
+    c = {n: T.col[:, i:i + 1] for i, n in enumerate(names)}
+    mineA = T.landA[:, 4 * rank:4 * rank + 1]
+    mineB = T.landB[:, 4 * rank:4 * rank + 2]
+    all_in = K_ENG * (N - 1)
+
+    Y.dma_start(T.xs[:], T.x[:]).then_inc(S.ldx, 16)
+    C.dma_start(T.vs[:], T.v[:]).then_inc(S.ldv, 16)
+    V.memset(T.wd[:, 0:1], 1.0 / D).then_inc(S.cw, 1)
+    V.memset(T.wd[:, 1:2], 2.0 / D).then_inc(S.cw, 1)
+    V.memset(T.ones[:], 1.0).then_inc(S.cone, 1)
+    g.wait_ge(S.cone, 1)
+    g.affine_select(T.ident[:], T.ones[:], [[-1, 128]], A.is_equal, 0.0, 0, 1).then_inc(S.cid, 1)
+
+    C.wait_ge(S.ldx, 16)
+    C.activation(T.pr[:, 0:128], T.xs[:], F.Square).then_inc(S.pxx, 1)
+    C.wait_ge(S.ldv, 16)
+    C.activation(T.pr[:, 256:384], T.vs[:], F.Square).then_inc(S.pvv, 1)
+
+    P.wait_ge(S.cw, 2)
+    P.wait_ge(S.pxx, 1)
+    P.matmul(T.psa[:, 0:1], T.pr[:, 0:128], T.wd[:, 0:1], True, True).then_inc(S.sta, 1)
+    P.wait_ge(S.pvv, 1)
+    P.matmul(T.psb[:, 1:2], T.pr[:, 256:384], T.wd[:, 0:1], True, True).then_inc(S.stb, 1)
+    P.wait_ge(S.pxv, 1)
+    P.matmul(T.psb[:, 0:1], T.pr[:, 128:256], T.wd[:, 1:2], True, True).then_inc(S.stb, 1)
+
+    V.wait_ge(S.sta, 1)
+    V.tensor_copy(mineA, T.psa[:, 0:1]).then_inc(S.minea, 1)
+    V.wait_ge(S.ldx, 16)
+    V.wait_ge(S.ldv, 16)
+    V.tensor_tensor(T.pr[:, 128:256], T.xs[:], T.vs[:], A.mult).then_inc(S.pxv, 1)
+    V.wait_ge(S.stb, 2)
+    V.tensor_copy(mineB, T.psb[:, 0:2]).then_inc(S.mineb, 1)
+
+    sent = 0
+    hs = [h for h, _ in helpers]
+    g.wait_ge(S.minea, 1)
+    sent += _send(g, T, topo, core, hs, mineA, S.arra)
+    sent += _send(g, T, topo, core, direct, mineA, S.arra)
+    g.wait_ge(S.mineb, 1)
+    sent += _send(g, T, topo, core, hs, mineB, S.arrb)
+    sent += _send(g, T, topo, core, direct, mineB, S.arrb)
+
+    P.wait_ge(S.cid, 1)
+    P.wait_ge(S.ldx, 16)
+    P.transpose(T.pxt[:, 0:128], T.xs[:], T.ident[:]).then_inc(S.tx, 1)
+    P.wait_ge(S.ldv, 16)
+    P.transpose(T.pvt[:, 0:128], T.vs[:], T.ident[:]).then_inc(S.tv, 1)
+
+    V.wait_ge(S.arra, all_in)
+    V.wait_ge(S.minea, 1)
+    V.tensor_reduce(c["m1"], T.landA[:, 0:4 * N:4], X, A.add).then_inc(S.m1, 1)
+    C.wait_ge(S.m1, 1)
+    C.activation(c["s1"], c["m1"], F.Sqrt, bias=EPS).then_inc(S.s1, 1)
+    V.wait_ge(S.m1, 1)
+    V.tensor_scalar(c["a1"], c["m1"], EPS, None, A.add).then_inc(S.a1, 1)
+    V.wait_ge(S.a1, 1)
+    V.reciprocal(c["q1"], c["a1"]).then_inc(S.q1, 1)
+    V.wait_ge(S.q1, 1)
+    V.tensor_scalar(c["qh1"], c["q1"], -0.5, None, A.mult).then_inc(S.qh1, 1)
+    V.wait_ge(S.arrb, all_in)
+    V.wait_ge(S.mineb, 1)
+    V.tensor_reduce(c["c2"], T.landB[:, 0:4 * N:4], X, A.add).then_inc(S.c2, 1)
+    V.tensor_reduce(c["mv"], T.landB[:, 1:4 * N:4], X, A.add).then_inc(S.mv, 1)
+    V.wait_ge(S.mv, 1)
+    V.tensor_scalar(c["mve"], c["mv"], EPS, None, A.add).then_inc(S.mve, 1)
+    C.wait_ge(S.s1, 1)
+    C.wait_ge(S.q1, 1)
+    C.activation(c["u1"], c["s1"], F.Copy, scale=c["q1"]).then_inc(S.u1, 1)
+    V.wait_ge(S.s1, 1)
+    V.wait_ge(S.qh1, 1)
+    V.tensor_scalar(c["g1"], c["s1"], c["qh1"], c["s1"], A.mult, A.mult).then_inc(S.g1, 1)
+    V.wait_ge(S.g1, 1)
+    V.wait_ge(S.u1, 1)
+    V.tensor_scalar(c["r1"], c["g1"], 1.5, c["u1"], A.add, A.mult).then_inc(S.r1, 1)
+
+    C.wait_ge(S.r1, 1)
+    C.wait_ge(S.tx, 1)
+    C.activation(T.xr[:], T.pxt[:, 0:128], F.Copy, scale=c["r1"]).then_inc(S.xrs, 1)
+    V.wait_ge(S.r1, 1)
+    V.wait_ge(S.c2, 1)
+    V.tensor_scalar(c["tt"], c["r1"], c["m1"], c["c2"], A.mult, A.add).then_inc(S.tt, 1)
+    V.wait_ge(S.tt, 1)
+    V.wait_ge(S.mve, 1)
+    V.tensor_scalar(c["a2"], c["tt"], c["r1"], c["mve"], A.mult, A.add).then_inc(S.a2, 1)
+    C.wait_ge(S.a2, 1)
+    C.activation(c["s2"], c["a2"], F.Sqrt).then_inc(S.s2, 1)
+    C.wait_ge(S.s2, 1)
+    C.activation(c["sh2"], c["s2"], F.Copy, scale=-0.5).then_inc(S.sh2, 1)
+    V.wait_ge(S.a2, 1)
+    V.reciprocal(c["q2"], c["a2"]).then_inc(S.q2, 1)
+    C.wait_ge(S.q2, 1)
+    C.activation(c["u2"], c["s2"], F.Copy, scale=c["q2"]).then_inc(S.u2, 1)
+    C.wait_ge(S.u2, 1)
+    C.wait_ge(S.sh2, 1)
+    C.activation(c["w2"], c["u2"], F.Identity, bias=1.5, scale=c["sh2"]).then_inc(S.w2, 1)
+    V.wait_ge(S.xrs, 1)
+    V.wait_ge(S.tv, 1)
+    V.tensor_tensor(T.zt[:], T.xr[:], T.pvt[:, 0:128], A.add).then_inc(S.zs, 1)
+    V.wait_ge(S.u2, 1)
+    V.wait_ge(S.w2, 1)
+    V.wait_ge(S.cid, 1)
+    V.tensor_scalar(T.dg[:], T.ident[:], c["u2"], c["w2"], A.mult, A.mult).then_inc(S.dgs, 1)
+
+    P.wait_ge(S.zs, 1)
+    P.wait_ge(S.dgs, 1)
+    P.matmul(T.pya[:, 0:64], T.zt[:], T.dg[:, 0:64], True, True).then_inc(S.ya, 1)
+    P.matmul(T.pyb[:, 0:64], T.zt[:], T.dg[:, 64:128], True, True).then_inc(S.yb, 1)
+    C.wait_ge(S.ya, 1)
+    C.activation(T.ys[:, 0:64], T.pya[:, 0:64], F.Copy).then_inc(S.ca, 1)
+    V.wait_ge(S.yb, 1)
+    V.tensor_copy(T.ys[:, 64:128], T.pyb[:, 0:64]).then_inc(S.cb, 1)
+    Y.wait_ge(S.ca, 1)
+    Y.wait_ge(S.cb, 1)
+    Y.dma_start(T.y[:], T.ys[:]).then_inc(S.out, 16)
+    Y.wait_ge(S.out, 16)
+    g.wait_ge(S.sent, sent)

@@ -5,7 +5,9 @@ N = 6
 D = 128 * N
 EPS = 0.01
 SIM_CORES = 256
-K_ENG = 8
+K_ON = 8
+K_OFF = 8
+K_DIR = 8
 PER_HELPER = 2
 
 SCRATCH = {
@@ -15,26 +17,26 @@ SCRATCH = {
     "wd": ("sbuf", [128, 2], "float32"),
     "ones": ("sbuf", [128, 128], "float32"),
     "ident": ("sbuf", [128, 128], "float32"),
-    "landA": ("sbuf", [128, 4 * N], "float32"),
-    "landB": ("sbuf", [128, 4 * N], "float32"),
+    "mine": ("sbuf", [128, 3], "float32"),
+    "land": ("sbuf", [128, 4 * N], "float32"),
     "col": ("sbuf", [128, 32], "float32"),
     "xr": ("sbuf", [128, 128], "float32"),
     "zt": ("sbuf", [128, 128], "float32"),
     "dg": ("sbuf", [128, 128], "float32"),
     "ys": ("sbuf", [128, 128], "float32"),
-    "psa": ("psum", [128, 512], "float32"),
-    "psb": ("psum", [128, 512], "float32"),
+    "pst": ("psum", [128, 512], "float32"),
     "pxt": ("psum", [128, 512], "float32"),
     "pvt": ("psum", [128, 512], "float32"),
     "pya": ("psum", [128, 512], "float32"),
     "pyb": ("psum", [128, 512], "float32"),
 }
-SEMAPHORES = ["ldx", "ldv", "cw", "cone", "cid", "pxx", "pxv", "pvv", "sta", "stb", "minea", "mineb", "tx", "tv",
-              "arra", "arrb", "sent", "m1", "a1", "q1", "qh1", "c2", "mv", "mve", "s1", "u1", "g1", "r1", "xrs", "tt", "a2",
-              "q2", "s2", "sh2", "u2", "w2", "zs", "dgs", "ya", "yb", "ca", "cb", "out"]
+COLS = ["ap", "qp", "qhp", "sp", "up", "gp", "rp", "dl", "rho", "sr", "shr", "qr", "ur", "wr",
+        "m1", "c2", "mve", "r1", "tt", "a2", "q2", "s2", "sh2", "u2", "w2"]
+SEMAPHORES = ["ldx", "ldv", "cw", "cone", "cid", "pxx", "pxv", "pvv", "st", "mines", "own", "tx", "tv",
+              "arr", "sent", "xrs", "zs", "dgs", "ya", "yb", "ca", "cb", "outa", "outb"] + ["k_" + n for n in COLS]
 
 
-def _low_bits(mask, k):
+def _some_bits(mask, k):
     got, bit = 0, 1
     while k > 0:
         if mask & bit:
@@ -53,53 +55,60 @@ def _plan(rank_core, cores, topo):
             and all(topo.may_write(c, d) for d in cross)]
     cand.sort(key=lambda c: (topo.die(c) != topo.die(rank_core), c))
     groups = [cross[i:i + PER_HELPER] for i in range(0, len(cross), PER_HELPER)]
-    return direct, [(cand[i], grp) for i, grp in enumerate(groups)]
+    return direct, cross, [(cand[i], grp) for i, grp in enumerate(groups)]
 
 
-def _send(g, T, topo, core, dests, ap, sem):
-    m = topo.mask(core, dests[0])
-    for d in dests:
-        m &= topo.mask(core, d)
-    m = _low_bits(m, K_ENG)
+def _send(g, T, topo, core, dests, src, dst, sem, k):
+    mask = _some_bits(min(topo.mask(core, d) for d in dests), k)
     ids = []
     for d in dests:
         rid, pid = topo.addr(d, core)
         ids.append(DstId(rid=rid, pnc=pid))
-    g.remote_dma_fused([RemoteDMATransfer(dst_ids=ids, dma_engine_mask=m, remote_sem=sem, srcs=[ap],
-                                          dsts=[ap for _ in dests], alu_op=0)], local_sem=T.sem.sent)
-    return K_ENG
+    g.remote_dma_fused([RemoteDMATransfer(dst_ids=ids, dma_engine_mask=mask, remote_sem=sem, srcs=[src],
+                                          dsts=[dst for _ in dests], alu_op=0)], local_sem=T.sem.sent)
 
 
 def rank_program(g, core, T, topo):
     S = T.sem
     cores = list(T.cores)
     rank = T.rank_of(core)
+
     if rank is None:
         for r, rc in enumerate(cores):
-            for h, grp in _plan(rc, cores, topo)[1]:
+            for h, grp in _plan(rc, cores, topo)[2]:
                 if h == core:
-                    sent = 0
-                    g.wait_ge(S.arra, K_ENG)
-                    sent += _send(g, T, topo, core, grp, T.landA[:, 4 * r:4 * r + 1], S.arra)
-                    g.wait_ge(S.arrb, K_ENG)
-                    sent += _send(g, T, topo, core, grp, T.landB[:, 4 * r:4 * r + 2], S.arrb)
-                    g.wait_ge(S.sent, sent)
+                    g.wait_ge(S.arr, K_ON)
+                    _send(g, T, topo, core, grp, T.mine[:], T.land[:, 4 * r:4 * r + 3], S.arr, K_OFF)
+                    g.wait_ge(S.sent, K_OFF)
         return
 
     A, F, X = AluOpType, ActivationFunctionType, AxisListType.X
     V, P, C, Y = g.vector, g.tensor, g.scalar, g.sync
-    direct, helpers = _plan(core, cores, topo)
-    names = ["m1", "a1", "q1", "qh1", "c2", "mv", "mve", "s1", "u1", "g1", "r1", "tt", "a2", "q2", "s2", "sh2", "u2", "w2"]
-    c = {n: T.col[:, i:i + 1] for i, n in enumerate(names)}
-    mineA = T.landA[:, 4 * rank:4 * rank + 1]
-    mineB = T.landB[:, 4 * rank:4 * rank + 2]
-    all_in = K_ENG * (N - 1)
+    direct, cross, helpers = _plan(core, cores, topo)
+    c = {n: T.col[:, i:i + 1] for i, n in enumerate(COLS)}
+    o = 4 * rank
+
+    def vw(*names):
+        for n in names:
+            V.wait_ge(S["k_" + n], 1)
+
+    def cwt(*names):
+        for n in names:
+            C.wait_ge(S["k_" + n], 1)
+
+    def ts(out, in0, s1, s2, op0, op1=None):
+        i = V.tensor_scalar(c[out], in0, s1, s2, op0) if op1 is None else V.tensor_scalar(c[out], in0, s1, s2, op0, op1)
+        i.then_inc(S["k_" + out], 1)
+
+    def act(out, in0, func, **kw):
+        C.activation(c[out], c[in0], func, **kw).then_inc(S["k_" + out], 1)
 
     Y.dma_start(T.xs[:], T.x[:]).then_inc(S.ldx, 16)
     C.dma_start(T.vs[:], T.v[:]).then_inc(S.ldv, 16)
     V.memset(T.wd[:, 0:1], 1.0 / D).then_inc(S.cw, 1)
     V.memset(T.wd[:, 1:2], 2.0 / D).then_inc(S.cw, 1)
     V.memset(T.ones[:], 1.0).then_inc(S.cone, 1)
+    V.memset(T.land[:, o:o + 1], 0.0).then_inc(S.own, 1)
     g.wait_ge(S.cone, 1)
     g.affine_select(T.ident[:], T.ones[:], [[-1, 128]], A.is_equal, 0.0, 0, 1).then_inc(S.cid, 1)
 
@@ -107,31 +116,25 @@ def rank_program(g, core, T, topo):
     C.activation(T.pr[:, 0:128], T.xs[:], F.Square).then_inc(S.pxx, 1)
     C.wait_ge(S.ldv, 16)
     C.activation(T.pr[:, 256:384], T.vs[:], F.Square).then_inc(S.pvv, 1)
-
-    P.wait_ge(S.cw, 2)
-    P.wait_ge(S.pxx, 1)
-    P.matmul(T.psa[:, 0:1], T.pr[:, 0:128], T.wd[:, 0:1], True, True).then_inc(S.sta, 1)
-    P.wait_ge(S.pvv, 1)
-    P.matmul(T.psb[:, 1:2], T.pr[:, 256:384], T.wd[:, 0:1], True, True).then_inc(S.stb, 1)
-    P.wait_ge(S.pxv, 1)
-    P.matmul(T.psb[:, 0:1], T.pr[:, 128:256], T.wd[:, 1:2], True, True).then_inc(S.stb, 1)
-
-    V.wait_ge(S.sta, 1)
-    V.tensor_copy(mineA, T.psa[:, 0:1]).then_inc(S.minea, 1)
     V.wait_ge(S.ldx, 16)
     V.wait_ge(S.ldv, 16)
     V.tensor_tensor(T.pr[:, 128:256], T.xs[:], T.vs[:], A.mult).then_inc(S.pxv, 1)
-    V.wait_ge(S.stb, 2)
-    V.tensor_copy(mineB, T.psb[:, 0:2]).then_inc(S.mineb, 1)
 
-    sent = 0
+    P.wait_ge(S.cw, 2)
+    P.wait_ge(S.pxx, 1)
+    P.matmul(T.pst[:, 0:1], T.pr[:, 0:128], T.wd[:, 0:1], True, True).then_inc(S.st, 1)
+    P.wait_ge(S.pvv, 1)
+    P.matmul(T.pst[:, 2:3], T.pr[:, 256:384], T.wd[:, 0:1], True, True).then_inc(S.st, 1)
+    P.wait_ge(S.pxv, 1)
+    P.matmul(T.pst[:, 1:2], T.pr[:, 128:256], T.wd[:, 1:2], True, True).then_inc(S.st, 1)
+
+    V.wait_ge(S.st, 3)
+    V.tensor_copy(T.mine[:], T.pst[:, 0:3]).then_inc(S.mines, 1)
+
     hs = [h for h, _ in helpers]
-    g.wait_ge(S.minea, 1)
-    sent += _send(g, T, topo, core, hs, mineA, S.arra)
-    sent += _send(g, T, topo, core, direct, mineA, S.arra)
-    g.wait_ge(S.mineb, 1)
-    sent += _send(g, T, topo, core, hs, mineB, S.arrb)
-    sent += _send(g, T, topo, core, direct, mineB, S.arrb)
+    g.wait_ge(S.mines, 1)
+    _send(g, T, topo, core, hs, T.mine[:], T.mine[:], S.arr, K_ON)
+    _send(g, T, topo, core, direct, T.mine[:], T.land[:, o:o + 3], S.arr, K_DIR)
 
     P.wait_ge(S.cid, 1)
     P.wait_ge(S.ldx, 16)
@@ -139,58 +142,67 @@ def rank_program(g, core, T, topo):
     P.wait_ge(S.ldv, 16)
     P.transpose(T.pvt[:, 0:128], T.vs[:], T.ident[:]).then_inc(S.tv, 1)
 
-    V.wait_ge(S.arra, all_in)
-    V.wait_ge(S.minea, 1)
-    V.tensor_reduce(c["m1"], T.landA[:, 0:4 * N:4], X, A.add).then_inc(S.m1, 1)
-    C.wait_ge(S.m1, 1)
-    C.activation(c["s1"], c["m1"], F.Sqrt, bias=EPS).then_inc(S.s1, 1)
-    V.wait_ge(S.m1, 1)
-    V.tensor_scalar(c["a1"], c["m1"], EPS, None, A.add).then_inc(S.a1, 1)
-    V.wait_ge(S.a1, 1)
-    V.reciprocal(c["q1"], c["a1"]).then_inc(S.q1, 1)
-    V.wait_ge(S.q1, 1)
-    V.tensor_scalar(c["qh1"], c["q1"], -0.5, None, A.mult).then_inc(S.qh1, 1)
-    V.wait_ge(S.arrb, all_in)
-    V.wait_ge(S.mineb, 1)
-    V.tensor_reduce(c["c2"], T.landB[:, 0:4 * N:4], X, A.add).then_inc(S.c2, 1)
-    V.tensor_reduce(c["mv"], T.landB[:, 1:4 * N:4], X, A.add).then_inc(S.mv, 1)
-    V.wait_ge(S.mv, 1)
-    V.tensor_scalar(c["mve"], c["mv"], EPS, None, A.add).then_inc(S.mve, 1)
-    C.wait_ge(S.s1, 1)
-    C.wait_ge(S.q1, 1)
-    C.activation(c["u1"], c["s1"], F.Copy, scale=c["q1"]).then_inc(S.u1, 1)
-    V.wait_ge(S.s1, 1)
-    V.wait_ge(S.qh1, 1)
-    V.tensor_scalar(c["g1"], c["s1"], c["qh1"], c["s1"], A.mult, A.mult).then_inc(S.g1, 1)
-    V.wait_ge(S.g1, 1)
-    V.wait_ge(S.u1, 1)
-    V.tensor_scalar(c["r1"], c["g1"], 1.5, c["u1"], A.add, A.mult).then_inc(S.r1, 1)
+    V.tensor_copy(T.land[:, o + 1:o + 2], T.pst[:, 1:2]).then_inc(S.own, 1)
+    V.tensor_scalar(T.land[:, o + 2:o + 3], T.pst[:, 2:3], EPS, None, A.add).then_inc(S.own, 1)
+    V.wait_ge(S.mines, 1)
+    ts("ap", T.mine[:, 0:1], EPS, None, A.add)
+    cwt("ap")
+    act("sp", "ap", F.Sqrt)
+    vw("ap")
+    V.reciprocal(c["qp"], c["ap"]).then_inc(S.k_qp, 1)
+    vw("qp")
+    ts("qhp", c["qp"], -0.5, None, A.mult)
+    cwt("sp", "qp")
+    act("up", "sp", F.Copy, scale=c["qp"])
+    vw("sp", "qhp")
+    ts("gp", c["sp"], c["qhp"], c["sp"], A.mult, A.mult)
+    vw("gp", "up")
+    ts("rp", c["gp"], 1.5, c["up"], A.add, A.mult)
 
-    C.wait_ge(S.r1, 1)
+    V.wait_ge(S.arr, K_DIR * len(direct) + K_OFF * len(cross))
+    V.wait_ge(S.own, 3)
+    V.tensor_reduce(c["dl"], T.land[:, 0:4 * N:4], X, A.add).then_inc(S.k_dl, 1)
+    vw("dl")
+    ts("rho", c["dl"], c["qp"], 1.0, A.mult, A.add)
+    cwt("rho")
+    act("sr", "rho", F.Sqrt)
+    cwt("sr")
+    act("shr", "sr", F.Copy, scale=-0.5)
+    cwt("dl")
+    C.wait_ge(S.mines, 1)
+    act("m1", "dl", F.Identity, bias=T.mine[:, 0:1])
+    vw("rho")
+    V.reciprocal(c["qr"], c["rho"]).then_inc(S.k_qr, 1)
+    cwt("qr")
+    act("ur", "sr", F.Copy, scale=c["qr"])
+    cwt("ur", "shr")
+    act("wr", "ur", F.Identity, bias=1.5, scale=c["shr"])
+    V.tensor_reduce(c["c2"], T.land[:, 1:4 * N:4], X, A.add).then_inc(S.k_c2, 1)
+    V.tensor_reduce(c["mve"], T.land[:, 2:4 * N:4], X, A.add).then_inc(S.k_mve, 1)
+    vw("ur", "wr", "rp")
+    ts("r1", c["ur"], c["wr"], c["rp"], A.mult, A.mult)
+
+    cwt("r1")
     C.wait_ge(S.tx, 1)
     C.activation(T.xr[:], T.pxt[:, 0:128], F.Copy, scale=c["r1"]).then_inc(S.xrs, 1)
-    V.wait_ge(S.r1, 1)
-    V.wait_ge(S.c2, 1)
-    V.tensor_scalar(c["tt"], c["r1"], c["m1"], c["c2"], A.mult, A.add).then_inc(S.tt, 1)
-    V.wait_ge(S.tt, 1)
-    V.wait_ge(S.mve, 1)
-    V.tensor_scalar(c["a2"], c["tt"], c["r1"], c["mve"], A.mult, A.add).then_inc(S.a2, 1)
-    C.wait_ge(S.a2, 1)
-    C.activation(c["s2"], c["a2"], F.Sqrt).then_inc(S.s2, 1)
-    C.wait_ge(S.s2, 1)
-    C.activation(c["sh2"], c["s2"], F.Copy, scale=-0.5).then_inc(S.sh2, 1)
-    V.wait_ge(S.a2, 1)
-    V.reciprocal(c["q2"], c["a2"]).then_inc(S.q2, 1)
-    C.wait_ge(S.q2, 1)
-    C.activation(c["u2"], c["s2"], F.Copy, scale=c["q2"]).then_inc(S.u2, 1)
-    C.wait_ge(S.u2, 1)
-    C.wait_ge(S.sh2, 1)
-    C.activation(c["w2"], c["u2"], F.Identity, bias=1.5, scale=c["sh2"]).then_inc(S.w2, 1)
+    vw("r1", "c2", "m1")
+    ts("tt", c["r1"], c["m1"], c["c2"], A.mult, A.add)
+    vw("tt", "mve")
+    ts("a2", c["tt"], c["r1"], c["mve"], A.mult, A.add)
+    cwt("a2")
+    act("s2", "a2", F.Sqrt)
+    cwt("s2")
+    act("sh2", "s2", F.Copy, scale=-0.5)
+    vw("a2")
+    V.reciprocal(c["q2"], c["a2"]).then_inc(S.k_q2, 1)
+    cwt("q2")
+    act("u2", "s2", F.Copy, scale=c["q2"])
+    cwt("u2", "sh2")
+    act("w2", "u2", F.Identity, bias=1.5, scale=c["sh2"])
     V.wait_ge(S.xrs, 1)
     V.wait_ge(S.tv, 1)
     V.tensor_tensor(T.zt[:], T.xr[:], T.pvt[:, 0:128], A.add).then_inc(S.zs, 1)
-    V.wait_ge(S.u2, 1)
-    V.wait_ge(S.w2, 1)
+    vw("u2", "w2")
     V.wait_ge(S.cid, 1)
     V.tensor_scalar(T.dg[:], T.ident[:], c["u2"], c["w2"], A.mult, A.mult).then_inc(S.dgs, 1)
 
@@ -200,10 +212,12 @@ def rank_program(g, core, T, topo):
     P.matmul(T.pyb[:, 0:64], T.zt[:], T.dg[:, 64:128], True, True).then_inc(S.yb, 1)
     C.wait_ge(S.ya, 1)
     C.activation(T.ys[:, 0:64], T.pya[:, 0:64], F.Copy).then_inc(S.ca, 1)
+    C.wait_ge(S.ca, 1)
+    C.dma_start(T.y[:, 0:64], T.ys[:, 0:64]).then_inc(S.outa, 16)
     V.wait_ge(S.yb, 1)
     V.tensor_copy(T.ys[:, 64:128], T.pyb[:, 0:64]).then_inc(S.cb, 1)
-    Y.wait_ge(S.ca, 1)
     Y.wait_ge(S.cb, 1)
-    Y.dma_start(T.y[:], T.ys[:]).then_inc(S.out, 16)
-    Y.wait_ge(S.out, 16)
-    g.wait_ge(S.sent, sent)
+    Y.dma_start(T.y[:, 64:128], T.ys[:, 64:128]).then_inc(S.outb, 16)
+    C.wait_ge(S.outa, 16)
+    Y.wait_ge(S.outb, 16)
+    g.wait_ge(S.sent, K_ON + K_DIR)

@@ -1,3 +1,4 @@
+import math
 from concourse.bass import DstId, RemoteDMATransfer
 from concourse.mybir import AluOpType, AxisListType, ActivationFunctionType
 
@@ -17,23 +18,27 @@ SCRATCH = {
     "wd": ("sbuf", [128, 2], "float32"),
     "ones": ("sbuf", [128, 128], "float32"),
     "ident": ("sbuf", [128, 128], "float32"),
-    "mine": ("sbuf", [128, 3], "float32"),
+    "ma": ("sbuf", [128, 1], "float32"),
+    "mb": ("sbuf", [128, 2], "float32"),
     "land": ("sbuf", [128, 4 * N], "float32"),
+    "junk": ("sbuf", [128, 2 * N], "float32"),
     "col": ("sbuf", [128, 32], "float32"),
     "xr": ("sbuf", [128, 128], "float32"),
     "zt": ("sbuf", [128, 128], "float32"),
     "dg": ("sbuf", [128, 128], "float32"),
     "ys": ("sbuf", [128, 128], "float32"),
+    "psa": ("psum", [128, 512], "float32"),
     "pst": ("psum", [128, 512], "float32"),
     "pxt": ("psum", [128, 512], "float32"),
     "pvt": ("psum", [128, 512], "float32"),
     "pya": ("psum", [128, 512], "float32"),
     "pyb": ("psum", [128, 512], "float32"),
 }
-COLS = ["ap", "qp", "qhp", "sp", "up", "gp", "rp", "dl", "rho", "sr", "shr", "qr", "ur", "wr",
-        "m1", "c2", "mve", "r1", "tt", "a2", "q2", "s2", "sh2", "u2", "w2"]
-SEMAPHORES = ["ldx", "ldv", "cw", "cone", "cid", "pxx", "pxv", "pvv", "st", "mines", "own", "tx", "tv",
-              "arr", "sent", "xrs", "zs", "dgs", "ya", "yb", "ca", "cb", "outa", "outb"] + ["k_" + n for n in COLS]
+COLS = ["sp", "qp", "sph", "spn", "a1", "q1", "sr", "h1", "s1n", "wn1", "m1", "c2", "mve", "r1", "tt",
+        "a2", "q2", "s2", "sh2", "u2", "w2"]
+SEMAPHORES = ["ldx", "ldv", "cw", "cone", "cid", "pxx", "pxv", "pvv", "sta", "stb", "mas", "mbs", "owna", "ownb", "tx", "tv",
+              "arra", "arrb", "sent", "xrs", "zs", "dga", "dgb", "ya", "yb", "ca", "cb", "outa", "outb"] \
+    + ["k_" + n for n in COLS]
 
 
 def _some_bits(mask, k):
@@ -77,9 +82,11 @@ def rank_program(g, core, T, topo):
         for r, rc in enumerate(cores):
             for h, grp in _plan(rc, cores, topo)[2]:
                 if h == core:
-                    g.wait_ge(S.arr, K_ON)
-                    _send(g, T, topo, core, grp, T.mine[:], T.land[:, 4 * r:4 * r + 3], S.arr, K_OFF)
-                    g.wait_ge(S.sent, K_OFF)
+                    g.wait_ge(S.arra, K_ON)
+                    _send(g, T, topo, core, grp, T.ma[:], T.land[:, 4 * r:4 * r + 1], S.arra, K_OFF)
+                    g.wait_ge(S.arrb, K_ON)
+                    _send(g, T, topo, core, grp, T.mb[:], T.land[:, 4 * r + 1:4 * r + 3], S.arrb, K_OFF)
+                    g.wait_ge(S.sent, 2 * K_OFF)
         return
 
     A, F, X = AluOpType, ActivationFunctionType, AxisListType.X
@@ -87,6 +94,7 @@ def rank_program(g, core, T, topo):
     direct, cross, helpers = _plan(core, cores, topo)
     c = {n: T.col[:, i:i + 1] for i, n in enumerate(COLS)}
     o = 4 * rank
+    landed = K_DIR * len(direct) + K_OFF * len(cross)
 
     def vw(*names):
         for n in names:
@@ -103,84 +111,81 @@ def rank_program(g, core, T, topo):
     def act(out, in0, func, **kw):
         C.activation(c[out], c[in0], func, **kw).then_inc(S["k_" + out], 1)
 
-    Y.dma_start(T.xs[:], T.x[:]).then_inc(S.ldx, 16)
-    C.dma_start(T.vs[:], T.v[:]).then_inc(S.ldv, 16)
+    Y.dma_start(T.xs[0:64, :], T.x[0:64, :]).then_inc(S.ldx, 16)
+    C.dma_start(T.xs[64:128, :], T.x[64:128, :]).then_inc(S.ldx, 16)
+    Y.dma_start(T.vs[0:64, :], T.v[0:64, :]).then_inc(S.ldv, 16)
+    C.dma_start(T.vs[64:128, :], T.v[64:128, :]).then_inc(S.ldv, 16)
     V.memset(T.wd[:, 0:1], 1.0 / D).then_inc(S.cw, 1)
     V.memset(T.wd[:, 1:2], 2.0 / D).then_inc(S.cw, 1)
     V.memset(T.ones[:], 1.0).then_inc(S.cone, 1)
-    V.memset(T.land[:, o:o + 1], 0.0).then_inc(S.own, 1)
     g.wait_ge(S.cone, 1)
     g.affine_select(T.ident[:], T.ones[:], [[-1, 128]], A.is_equal, 0.0, 0, 1).then_inc(S.cid, 1)
 
-    C.wait_ge(S.ldx, 16)
+    C.wait_ge(S.ldx, 32)
     C.activation(T.pr[:, 0:128], T.xs[:], F.Square).then_inc(S.pxx, 1)
-    C.wait_ge(S.ldv, 16)
+    C.wait_ge(S.ldv, 32)
     C.activation(T.pr[:, 256:384], T.vs[:], F.Square).then_inc(S.pvv, 1)
-    V.wait_ge(S.ldx, 16)
-    V.wait_ge(S.ldv, 16)
-    V.tensor_tensor(T.pr[:, 128:256], T.xs[:], T.vs[:], A.mult).then_inc(S.pxv, 1)
 
     P.wait_ge(S.cw, 2)
     P.wait_ge(S.pxx, 1)
-    P.matmul(T.pst[:, 0:1], T.pr[:, 0:128], T.wd[:, 0:1], True, True).then_inc(S.st, 1)
+    P.matmul(T.psa[:, 0:1], T.pr[:, 0:128], T.wd[:, 0:1], True, True).then_inc(S.sta, 1)
     P.wait_ge(S.pvv, 1)
-    P.matmul(T.pst[:, 2:3], T.pr[:, 256:384], T.wd[:, 0:1], True, True).then_inc(S.st, 1)
+    P.matmul(T.pst[:, 1:2], T.pr[:, 256:384], T.wd[:, 0:1], True, True).then_inc(S.stb, 1)
     P.wait_ge(S.pxv, 1)
-    P.matmul(T.pst[:, 1:2], T.pr[:, 128:256], T.wd[:, 1:2], True, True).then_inc(S.st, 1)
+    P.matmul(T.pst[:, 0:1], T.pr[:, 128:256], T.wd[:, 1:2], True, True).then_inc(S.stb, 1)
 
-    V.wait_ge(S.st, 3)
-    V.tensor_copy(T.mine[:], T.pst[:, 0:3]).then_inc(S.mines, 1)
+    V.wait_ge(S.sta, 1)
+    V.tensor_copy(T.ma[:], T.psa[:, 0:1]).then_inc(S.mas, 1)
+    V.tensor_scalar(T.land[:, o:o + 1], T.psa[:, 0:1], EPS, None, A.add).then_inc(S.owna, 1)
+    V.wait_ge(S.ldx, 32)
+    V.wait_ge(S.ldv, 32)
+    V.tensor_tensor(T.pr[:, 128:256], T.xs[:], T.vs[:], A.mult).then_inc(S.pxv, 1)
+    V.wait_ge(S.owna, 1)
+    V.reciprocal(c["qp"], T.land[:, o:o + 1]).then_inc(S.k_qp, 1)
+    V.wait_ge(S.stb, 2)
+    V.tensor_copy(T.mb[:], T.pst[:, 0:2]).then_inc(S.mbs, 1)
+    V.tensor_copy(T.land[:, o + 1:o + 2], T.pst[:, 0:1]).then_inc(S.ownb, 1)
+    V.tensor_scalar(T.land[:, o + 2:o + 3], T.pst[:, 1:2], EPS, None, A.add).then_inc(S.ownb, 1)
 
     hs = [h for h, _ in helpers]
-    g.wait_ge(S.mines, 1)
-    _send(g, T, topo, core, hs, T.mine[:], T.mine[:], S.arr, K_ON)
-    _send(g, T, topo, core, direct, T.mine[:], T.land[:, o:o + 3], S.arr, K_DIR)
+    g.wait_ge(S.mas, 1)
+    _send(g, T, topo, core, hs, T.ma[:], T.ma[:], S.arra, K_ON)
+    g.wait_ge(S.mbs, 1)
+    _send(g, T, topo, core, hs, T.mb[:], T.mb[:], S.arrb, K_ON)
+    _send(g, T, topo, core, direct, T.ma[:], T.land[:, o:o + 1], S.arra, K_DIR)
+    _send(g, T, topo, core, direct, T.mb[:], T.land[:, o + 1:o + 3], S.arrb, K_DIR)
 
     P.wait_ge(S.cid, 1)
-    P.wait_ge(S.ldx, 16)
+    P.wait_ge(S.ldx, 32)
     P.transpose(T.pxt[:, 0:128], T.xs[:], T.ident[:]).then_inc(S.tx, 1)
-    P.wait_ge(S.ldv, 16)
+    P.wait_ge(S.ldv, 32)
     P.transpose(T.pvt[:, 0:128], T.vs[:], T.ident[:]).then_inc(S.tv, 1)
 
-    V.tensor_copy(T.land[:, o + 1:o + 2], T.pst[:, 1:2]).then_inc(S.own, 1)
-    V.tensor_scalar(T.land[:, o + 2:o + 3], T.pst[:, 2:3], EPS, None, A.add).then_inc(S.own, 1)
-    V.wait_ge(S.mines, 1)
-    ts("ap", T.mine[:, 0:1], EPS, None, A.add)
-    cwt("ap")
-    act("sp", "ap", F.Sqrt)
-    vw("ap")
-    V.reciprocal(c["qp"], c["ap"]).then_inc(S.k_qp, 1)
-    vw("qp")
-    ts("qhp", c["qp"], -0.5, None, A.mult)
-    cwt("sp", "qp")
-    act("up", "sp", F.Copy, scale=c["qp"])
-    vw("sp", "qhp")
-    ts("gp", c["sp"], c["qhp"], c["sp"], A.mult, A.mult)
-    vw("gp", "up")
-    ts("rp", c["gp"], 1.5, c["up"], A.add, A.mult)
+    C.wait_ge(S.owna, 1)
+    C.activation(c["sp"], T.land[:, o:o + 1], F.Sqrt).then_inc(S.k_sp, 1)
+    cwt("sp")
+    act("sph", "sp", F.Copy, scale=math.sqrt(0.5))
+    act("spn", "sp", F.Copy, scale=-1.0)
 
-    V.wait_ge(S.arr, K_DIR * len(direct) + K_OFF * len(cross))
-    V.wait_ge(S.own, 3)
-    V.tensor_reduce(c["dl"], T.land[:, 0:4 * N:4], X, A.add).then_inc(S.k_dl, 1)
-    vw("dl")
-    ts("rho", c["dl"], c["qp"], 1.0, A.mult, A.add)
-    cwt("rho")
-    act("sr", "rho", F.Sqrt)
-    cwt("sr")
-    act("shr", "sr", F.Copy, scale=-0.5)
-    cwt("dl")
-    C.wait_ge(S.mines, 1)
-    act("m1", "dl", F.Identity, bias=T.mine[:, 0:1])
-    vw("rho")
-    V.reciprocal(c["qr"], c["rho"]).then_inc(S.k_qr, 1)
-    cwt("qr")
-    act("ur", "sr", F.Copy, scale=c["qr"])
-    cwt("ur", "shr")
-    act("wr", "ur", F.Identity, bias=1.5, scale=c["shr"])
-    V.tensor_reduce(c["c2"], T.land[:, 1:4 * N:4], X, A.add).then_inc(S.k_c2, 1)
-    V.tensor_reduce(c["mve"], T.land[:, 2:4 * N:4], X, A.add).then_inc(S.k_mve, 1)
-    vw("ur", "wr", "rp")
-    ts("r1", c["ur"], c["wr"], c["rp"], A.mult, A.mult)
+    V.wait_ge(S.arra, landed)
+    V.tensor_reduce(c["a1"], T.land[:, 0:4 * N:4], X, A.add).then_inc(S.k_a1, 1)
+    vw("a1")
+    V.reciprocal(c["q1"], c["a1"]).then_inc(S.k_q1, 1)
+    cwt("a1", "qp")
+    act("sr", "a1", F.Sqrt, scale=c["qp"])
+    cwt("sr", "sph", "spn")
+    act("h1", "sr", F.Square, scale=c["sph"])
+    act("s1n", "sr", F.Copy, scale=c["spn"])
+    act("m1", "a1", F.Identity, bias=-EPS)
+    vw("q1", "h1")
+    ts("wn1", c["q1"], c["h1"], -1.5, A.mult, A.add)
+    vw("wn1", "s1n")
+    ts("r1", c["wn1"], c["q1"], c["s1n"], A.mult, A.mult)
+
+    C.wait_ge(S.arrb, landed)
+    C.wait_ge(S.ownb, 2)
+    C.activation(T.junk[:, 0:N], T.land[:, 1:4 * N:4], F.Copy, accum_out=c["c2"]).then_inc(S.k_c2, 1)
+    C.activation(T.junk[:, N:2 * N], T.land[:, 2:4 * N:4], F.Copy, accum_out=c["mve"]).then_inc(S.k_mve, 1)
 
     cwt("r1")
     C.wait_ge(S.tx, 1)
@@ -204,11 +209,13 @@ def rank_program(g, core, T, topo):
     V.tensor_tensor(T.zt[:], T.xr[:], T.pvt[:, 0:128], A.add).then_inc(S.zs, 1)
     vw("u2", "w2")
     V.wait_ge(S.cid, 1)
-    V.tensor_scalar(T.dg[:], T.ident[:], c["u2"], c["w2"], A.mult, A.mult).then_inc(S.dgs, 1)
+    V.tensor_scalar(T.dg[:, 0:64], T.ident[:, 0:64], c["u2"], c["w2"], A.mult, A.mult).then_inc(S.dga, 1)
+    V.tensor_scalar(T.dg[:, 64:128], T.ident[:, 64:128], c["u2"], c["w2"], A.mult, A.mult).then_inc(S.dgb, 1)
 
     P.wait_ge(S.zs, 1)
-    P.wait_ge(S.dgs, 1)
+    P.wait_ge(S.dga, 1)
     P.matmul(T.pya[:, 0:64], T.zt[:], T.dg[:, 0:64], True, True).then_inc(S.ya, 1)
+    P.wait_ge(S.dgb, 1)
     P.matmul(T.pyb[:, 0:64], T.zt[:], T.dg[:, 64:128], True, True).then_inc(S.yb, 1)
     C.wait_ge(S.ya, 1)
     C.activation(T.ys[:, 0:64], T.pya[:, 0:64], F.Copy).then_inc(S.ca, 1)
@@ -220,4 +227,4 @@ def rank_program(g, core, T, topo):
     Y.dma_start(T.y[:, 64:128], T.ys[:, 64:128]).then_inc(S.outb, 16)
     C.wait_ge(S.outa, 16)
     Y.wait_ge(S.outb, 16)
-    g.wait_ge(S.sent, K_ON + K_DIR)
+    g.wait_ge(S.sent, 2 * K_ON + 2 * K_DIR)

@@ -80,13 +80,22 @@ def rank_program(g, core, T, topo):
 
     if rank is None:
         for r, rc in enumerate(cores):
-            for h, grp in _plan(rc, cores, topo)[2]:
+            plan = _plan(rc, cores, topo)[2]
+            for h, grp in plan:
                 if h == core:
+                    hs = [hh for hh, _ in plan]
+                    w = 128 // len(hs)
+                    lo = w * hs.index(core)
+                    g.vector.memset(T.ones[:], 1.0).then_inc(S.cone, 1)
+                    g.wait_ge(S.cone, 1)
+                    g.affine_select(T.ident[:], T.ones[:], [[-1, 128]], AluOpType.is_equal, 0.0, 0, 1).then_inc(S.cid, 1)
+                    g.wait_ge(S.cid, 1)
+                    _send(g, T, topo, core, [rc], T.ident[:, lo:lo + w], T.ident[:, lo:lo + w], S.cid, K_OFF)
                     g.wait_ge(S.arra, K_ON)
                     _send(g, T, topo, core, grp, T.ma[:], T.land[:, 4 * r:4 * r + 1], S.arra, K_OFF)
                     g.wait_ge(S.arrb, K_ON)
                     _send(g, T, topo, core, grp, T.mb[:], T.land[:, 4 * r + 1:4 * r + 3], S.arrb, K_OFF)
-                    g.wait_ge(S.sent, 2 * K_OFF)
+                    g.wait_ge(S.sent, 3 * K_OFF)
         return
 
     A, F, X = AluOpType, ActivationFunctionType, AxisListType.X
@@ -95,6 +104,7 @@ def rank_program(g, core, T, topo):
     c = {n: T.col[:, i:i + 1] for i, n in enumerate(COLS)}
     o = 4 * rank
     landed = K_DIR * len(direct) + K_OFF * len(cross)
+    ident_in = K_OFF * len(helpers)
 
     def vw(*names):
         for n in names:
@@ -117,9 +127,6 @@ def rank_program(g, core, T, topo):
     C.dma_start(T.vs[64:128, :], T.v[64:128, :]).then_inc(S.ldv, 16)
     V.memset(T.wd[:, 0:1], 1.0 / D).then_inc(S.cw, 1)
     V.memset(T.wd[:, 1:2], 2.0 / D).then_inc(S.cw, 1)
-    V.memset(T.ones[:], 1.0).then_inc(S.cone, 1)
-    g.wait_ge(S.cone, 1)
-    g.affine_select(T.ident[:], T.ones[:], [[-1, 128]], A.is_equal, 0.0, 0, 1).then_inc(S.cid, 1)
 
     C.wait_ge(S.ldx, 32)
     C.activation(T.pr[:, 0:128], T.xs[:], F.Square).then_inc(S.pxx, 1)
@@ -155,7 +162,7 @@ def rank_program(g, core, T, topo):
     _send(g, T, topo, core, direct, T.ma[:], T.land[:, o:o + 1], S.arra, K_DIR)
     _send(g, T, topo, core, direct, T.mb[:], T.land[:, o + 1:o + 3], S.arrb, K_DIR)
 
-    P.wait_ge(S.cid, 1)
+    P.wait_ge(S.cid, ident_in)
     P.wait_ge(S.ldx, 32)
     P.transpose(T.pxt[:, 0:128], T.xs[:], T.ident[:]).then_inc(S.tx, 1)
     P.wait_ge(S.ldv, 32)
@@ -208,7 +215,7 @@ def rank_program(g, core, T, topo):
     V.wait_ge(S.tv, 1)
     V.tensor_tensor(T.zt[:], T.xr[:], T.pvt[:, 0:128], A.add).then_inc(S.zs, 1)
     vw("u2", "w2")
-    V.wait_ge(S.cid, 1)
+    V.wait_ge(S.cid, ident_in)
     V.tensor_scalar(T.dg[:, 0:64], T.ident[:, 0:64], c["u2"], c["w2"], A.mult, A.mult).then_inc(S.dga, 1)
     V.tensor_scalar(T.dg[:, 64:128], T.ident[:, 64:128], c["u2"], c["w2"], A.mult, A.mult).then_inc(S.dgb, 1)
 

@@ -16,8 +16,10 @@ SCRATCH = {
     "vs": ("sbuf", [128, 128], "float32"),
     "pr": ("sbuf", [128, 384], "float32"),
     "wd": ("sbuf", [128, 2], "float32"),
+    "kk": ("sbuf", [128, 6], "float32"),
     "ones": ("sbuf", [128, 128], "float32"),
     "ident": ("sbuf", [128, 128], "float32"),
+    "idk": ("sbuf", [128, 128], "float32"),
     "ma": ("sbuf", [128, 1], "float32"),
     "mb": ("sbuf", [128, 2], "float32"),
     "land": ("sbuf", [128, 4 * N], "float32"),
@@ -34,10 +36,9 @@ SCRATCH = {
     "pya": ("psum", [128, 512], "float32"),
     "pyb": ("psum", [128, 512], "float32"),
 }
-COLS = ["sp", "qp", "sph", "spn", "a1", "q1", "sr", "h1", "s1n", "wn1", "m1", "c2", "mve", "r1", "tt",
-        "a2", "q2", "s2", "sh2", "u2", "w2"]
-SEMAPHORES = ["ldx", "ldv", "cw", "cone", "cid", "pxx", "pxv", "pvv", "sta", "stb", "mas", "mbs", "owna", "ownb", "tx", "tv",
-              "arra", "arrb", "sent", "xrs", "zs", "dga", "dgb", "ya", "yb", "ca", "cb", "outa", "outb"] \
+COLS = ["sp", "qp", "sph", "a1", "h1", "sr", "spn", "q1", "wn1", "t1", "t2", "r1", "mv6", "b6", "a2", "q2", "s2", "u2", "w2"]
+SEMAPHORES = ["ldx", "ldv", "cw", "ck", "cone", "cid", "cik", "pxx", "pxv", "pvv", "sta", "stb", "owna", "ownb", "tx", "tv",
+              "arra", "arrb", "arrd", "sent", "xrs", "zs", "dga", "dgb", "ya", "yb", "ca", "cb", "outa", "outb"] \
     + ["k_" + n for n in COLS]
 
 
@@ -60,7 +61,8 @@ def _plan(rank_core, cores, topo):
             and all(topo.may_write(c, d) for d in cross)]
     cand.sort(key=lambda c: (topo.die(c) != topo.die(rank_core), c))
     groups = [cross[i:i + PER_HELPER] for i in range(0, len(cross), PER_HELPER)]
-    return direct, cross, [(cand[i], grp) for i, grp in enumerate(groups)]
+    n = len(groups)
+    return direct, cross, [(cand[i], grp) for i, grp in enumerate(groups)], [(cand[n + i], grp) for i, grp in enumerate(groups)]
 
 
 def _send(g, T, topo, core, dests, src, dst, sem, k):
@@ -80,31 +82,35 @@ def rank_program(g, core, T, topo):
 
     if rank is None:
         for r, rc in enumerate(cores):
-            plan = _plan(rc, cores, topo)[2]
-            for h, grp in plan:
-                if h == core:
-                    hs = [hh for hh, _ in plan]
-                    w = 128 // len(hs)
-                    lo = w * hs.index(core)
-                    g.vector.memset(T.ones[:], 1.0).then_inc(S.cone, 1)
-                    g.wait_ge(S.cone, 1)
-                    g.affine_select(T.ident[:], T.ones[:], [[-1, 128]], AluOpType.is_equal, 0.0, 0, 1).then_inc(S.cid, 1)
-                    g.wait_ge(S.cid, 1)
-                    _send(g, T, topo, core, [rc], T.ident[:, lo:lo + w], T.ident[:, lo:lo + w], S.cid, K_OFF)
-                    g.wait_ge(S.arra, K_ON)
-                    _send(g, T, topo, core, grp, T.ma[:], T.land[:, 4 * r:4 * r + 1], S.arra, K_OFF)
-                    g.wait_ge(S.arrb, K_ON)
-                    _send(g, T, topo, core, grp, T.mb[:], T.land[:, 4 * r + 1:4 * r + 3], S.arrb, K_OFF)
-                    g.wait_ge(S.sent, 3 * K_OFF)
+            _, _, pa, pb = _plan(rc, cores, topo)
+            hs = [hh for hh, _ in pa + pb]
+            for kind, plan in (("a", pa), ("b", pb)):
+                for h, grp in plan:
+                    if h == core:
+                        w = 128 // len(hs)
+                        lo = w * hs.index(core)
+                        g.vector.memset(T.ones[:], 1.0).then_inc(S.cone, 1)
+                        g.wait_ge(S.cone, 1)
+                        g.affine_select(T.ident[:], T.ones[:], [[-1, 128]], AluOpType.is_equal, 0.0, 0, 1).then_inc(S.cid, 1)
+                        g.wait_ge(S.cid, 1)
+                        _send(g, T, topo, core, [rc], T.ident[:, lo:lo + w], T.ident[:, lo:lo + w], S.cid, K_OFF)
+                        if kind == "a":
+                            g.wait_ge(S.arra, K_ON)
+                            _send(g, T, topo, core, grp, T.ma[:], T.land[:, 4 * r:4 * r + 1], S.arra, K_OFF)
+                        else:
+                            g.wait_ge(S.arrb, K_ON)
+                            _send(g, T, topo, core, grp, T.mb[:], T.land[:, 4 * r + 1:4 * r + 3], S.arrb, K_OFF)
+                        g.wait_ge(S.sent, 2 * K_OFF)
         return
 
     A, F, X = AluOpType, ActivationFunctionType, AxisListType.X
     V, P, C, Y = g.vector, g.tensor, g.scalar, g.sync
-    direct, cross, helpers = _plan(core, cores, topo)
+    direct, cross, helpa, helpb = _plan(core, cores, topo)
     c = {n: T.col[:, i:i + 1] for i, n in enumerate(COLS)}
     o = 4 * rank
-    landed = K_DIR * len(direct) + K_OFF * len(cross)
-    ident_in = K_OFF * len(helpers)
+    in_cross = K_OFF * len(cross)
+    in_direct = K_DIR * len(direct)
+    ident_in = K_OFF * (len(helpa) + len(helpb))
 
     def vw(*names):
         for n in names:
@@ -113,10 +119,6 @@ def rank_program(g, core, T, topo):
     def cwt(*names):
         for n in names:
             C.wait_ge(S["k_" + n], 1)
-
-    def ts(out, in0, s1, s2, op0, op1=None):
-        i = V.tensor_scalar(c[out], in0, s1, s2, op0) if op1 is None else V.tensor_scalar(c[out], in0, s1, s2, op0, op1)
-        i.then_inc(S["k_" + out], 1)
 
     def act(out, in0, func, **kw):
         C.activation(c[out], c[in0], func, **kw).then_inc(S["k_" + out], 1)
@@ -127,6 +129,9 @@ def rank_program(g, core, T, topo):
     C.dma_start(T.vs[64:128, :], T.v[64:128, :]).then_inc(S.ldv, 16)
     V.memset(T.wd[:, 0:1], 1.0 / D).then_inc(S.cw, 1)
     V.memset(T.wd[:, 1:2], 2.0 / D).then_inc(S.cw, 1)
+    V.memset(T.kk[:, 0:1], -1.5).then_inc(S.ck, 1)
+    V.memset(T.kk[:, 1:5], 0.0).then_inc(S.ck, 1)
+    V.memset(T.kk[:, 5:6], -1.5).then_inc(S.ck, 1)
 
     C.wait_ge(S.ldx, 32)
     C.activation(T.pr[:, 0:128], T.xs[:], F.Square).then_inc(S.pxx, 1)
@@ -142,25 +147,20 @@ def rank_program(g, core, T, topo):
     P.matmul(T.pst[:, 0:1], T.pr[:, 128:256], T.wd[:, 1:2], True, True).then_inc(S.stb, 1)
 
     V.wait_ge(S.sta, 1)
-    V.tensor_copy(T.ma[:], T.psa[:, 0:1]).then_inc(S.mas, 1)
-    V.tensor_scalar(T.land[:, o:o + 1], T.psa[:, 0:1], EPS, None, A.add).then_inc(S.owna, 1)
+    V.tensor_scalar(T.land[:, o:o + 1], T.psa[:, 0:1], EPS / N, None, A.add).then_inc(S.owna, 1)
     V.wait_ge(S.ldx, 32)
     V.wait_ge(S.ldv, 32)
     V.tensor_tensor(T.pr[:, 128:256], T.xs[:], T.vs[:], A.mult).then_inc(S.pxv, 1)
     V.wait_ge(S.owna, 1)
     V.reciprocal(c["qp"], T.land[:, o:o + 1]).then_inc(S.k_qp, 1)
     V.wait_ge(S.stb, 2)
-    V.tensor_copy(T.mb[:], T.pst[:, 0:2]).then_inc(S.mbs, 1)
-    V.tensor_copy(T.land[:, o + 1:o + 2], T.pst[:, 0:1]).then_inc(S.ownb, 1)
-    V.tensor_scalar(T.land[:, o + 2:o + 3], T.pst[:, 1:2], EPS, None, A.add).then_inc(S.ownb, 1)
+    V.tensor_copy(T.land[:, o + 1:o + 3], T.pst[:, 0:2]).then_inc(S.ownb, 1)
 
-    hs = [h for h, _ in helpers]
-    g.wait_ge(S.mas, 1)
-    _send(g, T, topo, core, hs, T.ma[:], T.ma[:], S.arra, K_ON)
-    g.wait_ge(S.mbs, 1)
-    _send(g, T, topo, core, hs, T.mb[:], T.mb[:], S.arrb, K_ON)
-    _send(g, T, topo, core, direct, T.ma[:], T.land[:, o:o + 1], S.arra, K_DIR)
-    _send(g, T, topo, core, direct, T.mb[:], T.land[:, o + 1:o + 3], S.arrb, K_DIR)
+    g.wait_ge(S.owna, 1)
+    _send(g, T, topo, core, [h for h, _ in helpa], T.land[:, o:o + 1], T.ma[:], S.arra, K_ON)
+    g.wait_ge(S.ownb, 1)
+    _send(g, T, topo, core, [h for h, _ in helpb], T.land[:, o + 1:o + 3], T.mb[:], S.arrb, K_ON)
+    _send(g, T, topo, core, direct, T.land[:, o:o + 3], T.land[:, o:o + 3], S.arrd, K_DIR)
 
     P.wait_ge(S.cid, ident_in)
     P.wait_ge(S.ldx, 32)
@@ -173,51 +173,49 @@ def rank_program(g, core, T, topo):
     cwt("sp")
     act("sph", "sp", F.Copy, scale=math.sqrt(0.5))
     act("spn", "sp", F.Copy, scale=-1.0)
+    C.wait_ge(S.cid, ident_in)
+    C.activation(T.idk[:], T.ident[:], F.Copy, scale=-math.sqrt(2.0)).then_inc(S.cik, 1)
 
-    V.wait_ge(S.arra, landed)
+    V.wait_ge(S.arra, in_cross)
+    V.wait_ge(S.arrd, in_direct)
     V.tensor_reduce(c["a1"], T.land[:, 0:4 * N:4], X, A.add).then_inc(S.k_a1, 1)
     vw("a1")
     V.reciprocal(c["q1"], c["a1"]).then_inc(S.k_q1, 1)
     cwt("a1", "qp")
     act("sr", "a1", F.Sqrt, scale=c["qp"])
-    cwt("sr", "sph", "spn")
+    cwt("sr", "sph")
     act("h1", "sr", F.Square, scale=c["sph"])
-    act("s1n", "sr", F.Copy, scale=c["spn"])
-    act("m1", "a1", F.Identity, bias=-EPS)
-    vw("q1", "h1")
-    ts("wn1", c["q1"], c["h1"], -1.5, A.mult, A.add)
-    vw("wn1", "s1n")
-    ts("r1", c["wn1"], c["q1"], c["s1n"], A.mult, A.mult)
+    C.wait_ge(S.arrb, in_cross)
+    C.wait_ge(S.arrd, in_direct)
+    C.wait_ge(S.ownb, 1)
+    C.activation(T.junk[:, 0:N], T.land[:, 2:4 * N:4], F.Identity, bias=(1.0 + EPS) / (N * N), scale=1.0 / N,
+                 accum_out=c["mv6"]).then_inc(S.k_mv6, 1)
+    i0, j0 = COLS.index("h1"), COLS.index("wn1")
+    vw("q1", "h1", "sr", "spn")
+    V.wait_ge(S.ck, 3)
+    V.tensor_tensor_scan(T.col[:, j0:j0 + 4], T.col[:, i0:i0 + 4], T.kk[:, 0:4], c["q1"], A.mult, A.add).then_inc(S.k_r1, 1)
+    vw("mv6")
+    V.tensor_scalar(c["b6"], c["q1"], -EPS / N, c["mv6"], A.mult, A.add).then_inc(S.k_b6, 1)
 
-    C.wait_ge(S.arrb, landed)
-    C.wait_ge(S.ownb, 2)
-    C.activation(T.junk[:, 0:N], T.land[:, 1:4 * N:4], F.Copy, accum_out=c["c2"]).then_inc(S.k_c2, 1)
-    C.activation(T.junk[:, N:2 * N], T.land[:, 2:4 * N:4], F.Copy, accum_out=c["mve"]).then_inc(S.k_mve, 1)
-
-    cwt("r1")
+    cwt("b6", "r1")
+    C.activation(T.junk[:, N:2 * N], T.land[:, 1:4 * N:4], F.Identity, bias=c["b6"], scale=c["r1"],
+                 accum_out=c["a2"]).then_inc(S.k_a2, 1)
+    cwt("a2")
+    act("s2", "a2", F.Sqrt, scale=0.5)
     C.wait_ge(S.tx, 1)
     C.activation(T.xr[:], T.pxt[:, 0:128], F.Copy, scale=c["r1"]).then_inc(S.xrs, 1)
-    vw("r1", "c2", "m1")
-    ts("tt", c["r1"], c["m1"], c["c2"], A.mult, A.add)
-    vw("tt", "mve")
-    ts("a2", c["tt"], c["r1"], c["mve"], A.mult, A.add)
-    cwt("a2")
-    act("s2", "a2", F.Sqrt)
-    cwt("s2")
-    act("sh2", "s2", F.Copy, scale=-0.5)
     vw("a2")
     V.reciprocal(c["q2"], c["a2"]).then_inc(S.k_q2, 1)
-    cwt("q2")
-    act("u2", "s2", F.Copy, scale=c["q2"])
-    cwt("u2", "sh2")
-    act("w2", "u2", F.Identity, bias=1.5, scale=c["sh2"])
+    i1, j1 = COLS.index("q2"), COLS.index("u2")
+    vw("q2", "s2")
+    V.tensor_tensor_scan(T.col[:, j1:j1 + 2], T.col[:, i1:i1 + 2], T.kk[:, 4:6], c["s2"], A.mult, A.add).then_inc(S.k_w2, 1)
     V.wait_ge(S.xrs, 1)
     V.wait_ge(S.tv, 1)
     V.tensor_tensor(T.zt[:], T.xr[:], T.pvt[:, 0:128], A.add).then_inc(S.zs, 1)
-    vw("u2", "w2")
-    V.wait_ge(S.cid, ident_in)
-    V.tensor_scalar(T.dg[:, 0:64], T.ident[:, 0:64], c["u2"], c["w2"], A.mult, A.mult).then_inc(S.dga, 1)
-    V.tensor_scalar(T.dg[:, 64:128], T.ident[:, 64:128], c["u2"], c["w2"], A.mult, A.mult).then_inc(S.dgb, 1)
+    vw("w2")
+    V.wait_ge(S.cik, 1)
+    V.tensor_scalar(T.dg[:, 0:64], T.idk[:, 0:64], c["u2"], c["w2"], A.mult, A.mult).then_inc(S.dga, 1)
+    V.tensor_scalar(T.dg[:, 64:128], T.idk[:, 64:128], c["u2"], c["w2"], A.mult, A.mult).then_inc(S.dgb, 1)
 
     P.wait_ge(S.zs, 1)
     P.wait_ge(S.dga, 1)
@@ -234,4 +232,4 @@ def rank_program(g, core, T, topo):
     Y.dma_start(T.y[:, 64:128], T.ys[:, 64:128]).then_inc(S.outb, 16)
     C.wait_ge(S.outa, 16)
     Y.wait_ge(S.outb, 16)
-    g.wait_ge(S.sent, 2 * K_ON + 2 * K_DIR)
+    g.wait_ge(S.sent, 2 * K_ON + K_DIR)

import math
from concourse.bass import DstId, RemoteDMATransfer
from concourse.mybir import AluOpType, AxisListType, ActivationFunctionType

N = 6
D = 128 * N
EPS = 0.01
SIM_CORES = 256
K_ON = 8
K_OFF = 8
K_DIR = 8
PER_HELPER = 2

SCRATCH = {
    "xs": ("sbuf", [128, 128], "float32"),
    "vs": ("sbuf", [128, 128], "float32"),
    "pr": ("sbuf", [128, 384], "float32"),
    "wd": ("sbuf", [128, 2], "float32"),
    "kk": ("sbuf", [128, 6], "float32"),
    "ones": ("sbuf", [128, 128], "float32"),
    "ident": ("sbuf", [128, 128], "float32"),
    "idk": ("sbuf", [128, 128], "float32"),
    "ma": ("sbuf", [128, 1], "float32"),
    "mb": ("sbuf", [128, 2], "float32"),
    "land": ("sbuf", [128, 4 * N], "float32"),
    "junk": ("sbuf", [128, 2 * N], "float32"),
    "col": ("sbuf", [128, 32], "float32"),
    "xr": ("sbuf", [128, 128], "float32"),
    "zt": ("sbuf", [128, 128], "float32"),
    "dg": ("sbuf", [128, 128], "float32"),
    "ys": ("sbuf", [128, 128], "float32"),
    "psa": ("psum", [128, 512], "float32"),
    "pst": ("psum", [128, 512], "float32"),
    "pxt": ("psum", [128, 512], "float32"),
    "pvt": ("psum", [128, 512], "float32"),
    "pya": ("psum", [128, 512], "float32"),
    "pyb": ("psum", [128, 512], "float32"),
}
COLS = ["sp", "qp", "sph", "a1", "h1", "sr", "spn", "q1", "wn1", "t1", "t2", "r1", "mv6", "b6", "a2", "q2", "s2", "u2", "w2"]
SEMAPHORES = ["ldx", "ldv", "cw", "ck", "cone", "cid", "cik", "pxx", "pxv", "pvv", "sta", "stb", "owna", "ownb", "tx", "tv",
              "arra", "arrb", "arrd", "sent", "xrs", "zs", "dga", "dgb", "ya", "yb", "ca", "cb", "outa", "outb"] \
    + ["k_" + n for n in COLS]


def _some_bits(mask, k):
    got, bit = 0, 1
    while k > 0:
        if mask & bit:
            got |= bit
            k -= 1
        bit <<= 1
    return got


def _plan(rank_core, cores, topo):
    others = [d for d in cores if d != rank_core]
    direct = [d for d in others if topo.may_write(rank_core, d)]
    cross = [d for d in others if not topo.may_write(rank_core, d)]
    cand = [c for c in range(SIM_CORES)
            if c not in cores and topo.host(c) == topo.host(rank_core) and topo.chip(c) == topo.chip(rank_core)
            and all(topo.may_write(c, d) for d in cross)]
    cand.sort(key=lambda c: (topo.die(c) != topo.die(rank_core), c))
    groups = [cross[i:i + PER_HELPER] for i in range(0, len(cross), PER_HELPER)]
    n = len(groups)
    return direct, cross, [(cand[i], grp) for i, grp in enumerate(groups)], [(cand[n + i], grp) for i, grp in enumerate(groups)]


def _send(g, T, topo, core, dests, src, dst, sem, k):
    mask = _some_bits(min(topo.mask(core, d) for d in dests), k)
    ids = []
    for d in dests:
        rid, pid = topo.addr(d, core)
        ids.append(DstId(rid=rid, pnc=pid))
    g.remote_dma_fused([RemoteDMATransfer(dst_ids=ids, dma_engine_mask=mask, remote_sem=sem, srcs=[src],
                                          dsts=[dst for _ in dests], alu_op=0)], local_sem=T.sem.sent)


def rank_program(g, core, T, topo):
    S = T.sem
    cores = list(T.cores)
    rank = T.rank_of(core)

    if rank is None:
        for r, rc in enumerate(cores):
            _, _, pa, pb = _plan(rc, cores, topo)
            hs = [hh for hh, _ in pa + pb]
            for kind, plan in (("a", pa), ("b", pb)):
                for h, grp in plan:
                    if h == core:
                        w = 128 // len(hs)
                        lo = w * hs.index(core)
                        g.vector.memset(T.ones[:], 1.0).then_inc(S.cone, 1)
                        g.wait_ge(S.cone, 1)
                        g.affine_select(T.ident[:], T.ones[:], [[-1, 128]], AluOpType.is_equal, 0.0, 0, 1).then_inc(S.cid, 1)
                        g.wait_ge(S.cid, 1)
                        _send(g, T, topo, core, [rc], T.ident[:, lo:lo + w], T.ident[:, lo:lo + w], S.cid, K_OFF)
                        if kind == "a":
                            g.wait_ge(S.arra, K_ON)
                            _send(g, T, topo, core, grp, T.ma[:], T.land[:, 4 * r:4 * r + 1], S.arra, K_OFF)
                        else:
                            g.wait_ge(S.arrb, K_ON)
                            _send(g, T, topo, core, grp, T.mb[:], T.land[:, 4 * r + 1:4 * r + 3], S.arrb, K_OFF)
                        g.wait_ge(S.sent, 2 * K_OFF)
        return

    A, F, X = AluOpType, ActivationFunctionType, AxisListType.X
    V, P, C, Y = g.vector, g.tensor, g.scalar, g.sync
    direct, cross, helpa, helpb = _plan(core, cores, topo)
    c = {n: T.col[:, i:i + 1] for i, n in enumerate(COLS)}
    o = 4 * rank
    in_cross = K_OFF * len(cross)
    in_direct = K_DIR * len(direct)
    ident_in = K_OFF * (len(helpa) + len(helpb))

    def vw(*names):
        for n in names:
            V.wait_ge(S["k_" + n], 1)

    def cwt(*names):
        for n in names:
            C.wait_ge(S["k_" + n], 1)

    def act(out, in0, func, **kw):
        C.activation(c[out], c[in0], func, **kw).then_inc(S["k_" + out], 1)

    Y.dma_start(T.xs[0:64, :], T.x[0:64, :]).then_inc(S.ldx, 16)
    C.dma_start(T.xs[64:128, :], T.x[64:128, :]).then_inc(S.ldx, 16)
    Y.dma_start(T.vs[0:64, :], T.v[0:64, :]).then_inc(S.ldv, 16)
    C.dma_start(T.vs[64:128, :], T.v[64:128, :]).then_inc(S.ldv, 16)
    V.memset(T.wd[:, 0:1], 1.0 / D).then_inc(S.cw, 1)
    V.memset(T.wd[:, 1:2], 2.0 / D).then_inc(S.cw, 1)
    V.memset(T.kk[:, 0:1], -1.5).then_inc(S.ck, 1)
    V.memset(T.kk[:, 1:5], 0.0).then_inc(S.ck, 1)
    V.memset(T.kk[:, 5:6], -1.5).then_inc(S.ck, 1)

    C.wait_ge(S.ldx, 32)
    C.activation(T.pr[:, 0:128], T.xs[:], F.Square).then_inc(S.pxx, 1)
    C.wait_ge(S.ldv, 32)
    C.activation(T.pr[:, 256:384], T.vs[:], F.Square).then_inc(S.pvv, 1)

    P.wait_ge(S.cw, 2)
    P.wait_ge(S.pxx, 1)
    P.matmul(T.psa[:, 0:1], T.pr[:, 0:128], T.wd[:, 0:1], True, True).then_inc(S.sta, 1)
    P.wait_ge(S.pvv, 1)
    P.matmul(T.pst[:, 1:2], T.pr[:, 256:384], T.wd[:, 0:1], True, True).then_inc(S.stb, 1)
    P.wait_ge(S.pxv, 1)
    P.matmul(T.pst[:, 0:1], T.pr[:, 128:256], T.wd[:, 1:2], True, True).then_inc(S.stb, 1)

    V.wait_ge(S.sta, 1)
    V.tensor_scalar(T.land[:, o:o + 1], T.psa[:, 0:1], EPS / N, None, A.add).then_inc(S.owna, 1)
    V.wait_ge(S.ldx, 32)
    V.wait_ge(S.ldv, 32)
    V.tensor_tensor(T.pr[:, 128:256], T.xs[:], T.vs[:], A.mult).then_inc(S.pxv, 1)
    V.wait_ge(S.owna, 1)
    V.reciprocal(c["qp"], T.land[:, o:o + 1]).then_inc(S.k_qp, 1)
    V.wait_ge(S.stb, 2)
    V.tensor_copy(T.land[:, o + 1:o + 3], T.pst[:, 0:2]).then_inc(S.ownb, 1)

    g.wait_ge(S.owna, 1)
    _send(g, T, topo, core, [h for h, _ in helpa], T.land[:, o:o + 1], T.ma[:], S.arra, K_ON)
    g.wait_ge(S.ownb, 1)
    _send(g, T, topo, core, [h for h, _ in helpb], T.land[:, o + 1:o + 3], T.mb[:], S.arrb, K_ON)
    _send(g, T, topo, core, direct, T.land[:, o:o + 3], T.land[:, o:o + 3], S.arrd, K_DIR)

    P.wait_ge(S.cid, ident_in)
    P.wait_ge(S.ldx, 32)
    P.transpose(T.pxt[:, 0:128], T.xs[:], T.ident[:]).then_inc(S.tx, 1)
    P.wait_ge(S.ldv, 32)
    P.transpose(T.pvt[:, 0:128], T.vs[:], T.ident[:]).then_inc(S.tv, 1)

    C.wait_ge(S.owna, 1)
    C.activation(c["sp"], T.land[:, o:o + 1], F.Sqrt).then_inc(S.k_sp, 1)
    cwt("sp")
    act("sph", "sp", F.Copy, scale=math.sqrt(0.5))
    act("spn", "sp", F.Copy, scale=-1.0)
    C.wait_ge(S.cid, ident_in)
    C.activation(T.idk[:], T.ident[:], F.Copy, scale=-math.sqrt(2.0)).then_inc(S.cik, 1)

    V.wait_ge(S.arra, in_cross)
    V.wait_ge(S.arrd, in_direct)
    V.tensor_reduce(c["a1"], T.land[:, 0:4 * N:4], X, A.add).then_inc(S.k_a1, 1)
    vw("a1")
    V.reciprocal(c["q1"], c["a1"]).then_inc(S.k_q1, 1)
    cwt("a1", "qp")
    act("sr", "a1", F.Sqrt, scale=c["qp"])
    cwt("sr", "sph")
    act("h1", "sr", F.Square, scale=c["sph"])
    C.wait_ge(S.arrb, in_cross)
    C.wait_ge(S.arrd, in_direct)
    C.wait_ge(S.ownb, 1)
    C.activation(T.junk[:, 0:N], T.land[:, 2:4 * N:4], F.Identity, bias=(1.0 + EPS) / (N * N), scale=1.0 / N,
                 accum_out=c["mv6"]).then_inc(S.k_mv6, 1)
    i0, j0 = COLS.index("h1"), COLS.index("wn1")
    vw("q1", "h1", "sr", "spn")
    V.wait_ge(S.ck, 3)
    V.tensor_tensor_scan(T.col[:, j0:j0 + 4], T.col[:, i0:i0 + 4], T.kk[:, 0:4], c["q1"], A.mult, A.add).then_inc(S.k_r1, 1)
    vw("mv6")
    V.tensor_scalar(c["b6"], c["q1"], -EPS / N, c["mv6"], A.mult, A.add).then_inc(S.k_b6, 1)

    cwt("b6", "r1")
    C.activation(T.junk[:, N:2 * N], T.land[:, 1:4 * N:4], F.Identity, bias=c["b6"], scale=c["r1"],
                 accum_out=c["a2"]).then_inc(S.k_a2, 1)
    cwt("a2")
    act("s2", "a2", F.Sqrt, scale=0.5)
    C.wait_ge(S.tx, 1)
    C.activation(T.xr[:], T.pxt[:, 0:128], F.Copy, scale=c["r1"]).then_inc(S.xrs, 1)
    vw("a2")
    V.reciprocal(c["q2"], c["a2"]).then_inc(S.k_q2, 1)
    i1, j1 = COLS.index("q2"), COLS.index("u2")
    vw("q2", "s2")
    V.tensor_tensor_scan(T.col[:, j1:j1 + 2], T.col[:, i1:i1 + 2], T.kk[:, 4:6], c["s2"], A.mult, A.add).then_inc(S.k_w2, 1)
    V.wait_ge(S.xrs, 1)
    V.wait_ge(S.tv, 1)
    V.tensor_tensor(T.zt[:], T.xr[:], T.pvt[:, 0:128], A.add).then_inc(S.zs, 1)
    vw("w2")
    V.wait_ge(S.cik, 1)
    V.tensor_scalar(T.dg[:, 0:64], T.idk[:, 0:64], c["u2"], c["w2"], A.mult, A.mult).then_inc(S.dga, 1)
    V.tensor_scalar(T.dg[:, 64:128], T.idk[:, 64:128], c["u2"], c["w2"], A.mult, A.mult).then_inc(S.dgb, 1)

    P.wait_ge(S.zs, 1)
    P.wait_ge(S.dga, 1)
    P.matmul(T.pya[:, 0:64], T.zt[:], T.dg[:, 0:64], True, True).then_inc(S.ya, 1)
    P.wait_ge(S.dgb, 1)
    P.matmul(T.pyb[:, 0:64], T.zt[:], T.dg[:, 64:128], True, True).then_inc(S.yb, 1)
    C.wait_ge(S.ya, 1)
    C.activation(T.ys[:, 0:64], T.pya[:, 0:64], F.Copy).then_inc(S.ca, 1)
    C.wait_ge(S.ca, 1)
    C.dma_start(T.y[:, 0:64], T.ys[:, 0:64]).then_inc(S.outa, 16)
    V.wait_ge(S.yb, 1)
    V.tensor_copy(T.ys[:, 64:128], T.pyb[:, 0:64]).then_inc(S.cb, 1)
    Y.wait_ge(S.cb, 1)
    Y.dma_start(T.y[:, 64:128], T.ys[:, 64:128]).then_inc(S.outb, 16)
    C.wait_ge(S.outa, 16)
    Y.wait_ge(S.outb, 16)
    g.wait_ge(S.sent, 2 * K_ON + K_DIR)
